import numpy as np
import ml_dtypes


def mxq(x, axis, fmt="e4m3"):
    dtype, down = {"e4m3": (ml_dtypes.float8_e4m3fn, 7), "e5m2": (ml_dtypes.float8_e5m2, 14)}[fmt]
    v = np.moveaxis(np.asarray(x, np.float32).astype(ml_dtypes.bfloat16).astype(np.float64), axis, -1)
    blocks = v.reshape(v.shape[:-1] + (-1, 32))
    amax = np.abs(blocks).max(-1, keepdims=True)
    byte = np.maximum(np.where(amax > 0, np.frexp(amax)[1] - 1 + 127, 0) - down, 1)
    scale = np.exp2(byte - 127.0)
    codes = (blocks / scale).astype(np.float32).astype(dtype).astype(np.float64)
    return np.moveaxis((codes * scale).reshape(v.shape), -1, axis)


WIDE = False


def mx_kscale(k):
    if not WIDE:
        return np.ones(k)
    levels = np.array([10, -10, 5, -5, 0])
    if k % 512:
        return np.exp2(np.random.permutation(np.resize(levels, k // 32))).repeat(32)
    a = np.empty((k // 512, 16))
    for p in range(k // 512):
        a[p, :8] = np.random.permutation(np.resize(levels, 8))
        for g in range(8):
            far = levels[np.abs(levels - a[p, g]) >= 10]
            a[p, g + 8] = far[np.random.randint(len(far))]
    return np.exp2(a.ravel()).repeat(32)


def f64(x):
    return np.asarray(x).astype(np.float64)


def striped(idx):
    return np.tile(np.asarray(idx).reshape(-1, 16).T, (8, 1)).astype(np.uint16)


def unstriped(offs):
    return offs[:16].T.reshape(-1).astype(np.int64)


E2M1 = np.array([0.0, 0.5, 1.0, 1.5, 2.0, 3.0, 4.0, 6.0, -0.0, -0.5, -1.0, -1.5, -2.0, -3.0, -4.0, -6.0])


def pack_weight(w, fmt):
    k, n = w.shape
    w = f64(np.asarray(w, np.float32).astype(ml_dtypes.bfloat16)).reshape(k // 32, 32, n)
    amax = np.abs(w).max(1)
    if fmt == "e4m3":
        byte = np.frexp(amax)[1] - 1 + 127 - 7
    else:
        mant, ex = np.frexp(amax / 6.0)
        byte = np.where(mant > 0.5, ex, ex - 1) + 127
    byte = np.clip(np.where(amax > 0, byte, 1), 1, 254)
    scaled = (w * np.exp2(127.0 - byte)[:, None, :]).reshape(k, n).astype(np.float32)
    by_word = np.ascontiguousarray(scaled.reshape(k // 512, 128, 4, n).transpose(0, 1, 3, 2))
    if fmt == "e4m3":
        words = by_word.astype(ml_dtypes.float8_e4m3fn).view(np.uint8)
    else:
        c = by_word.astype(ml_dtypes.float4_e2m1fn).view(np.uint8) & 0xF
        words = (c[..., 0::2] | (c[..., 1::2] << 4)).reshape(k // 512, 128, 2 * n)
    return np.ascontiguousarray(words), np.ascontiguousarray(byte.astype(np.uint8).reshape(k // 512, 16, n))


def unpack_weight(words, scales, fmt):
    g, _, n = scales.shape
    words = np.ascontiguousarray(words).reshape(g, 128, n, -1)
    if fmt == "e4m3":
        vals = words.view(ml_dtypes.float8_e4m3fn).astype(np.float64)
    else:
        nib = np.empty((g, 128, n, 4), np.uint8)
        nib[..., 0::2] = words & 0xF
        nib[..., 1::2] = words >> 4
        vals = E2M1[nib]
    vals = vals * np.repeat(np.exp2(scales.astype(np.float64) - 127.0), 8, axis=1)[..., None]
    return vals.transpose(0, 1, 3, 2).reshape(g * 512, n)


def sigmoid(v):
    return 1.0 / (1.0 + np.exp(-v))


D, T, I, Q, U, Z, M = 512, 2048, 512, 128, 1024, 1024, 2048


def setup_inputs():
    n = np.random.standard_normal
    idx = np.random.permutation(T)[:I]
    idx2 = np.random.permutation(U)[:I]
    idx3 = np.random.permutation(Z)[:I]
    idx4 = np.random.permutation(M)[:I]
    fd = mx_kscale(D)
    keysp = pack_weight(n((D, T)) / fd[:, None], "e2m1")
    return {
        "query": (n((D, Q)) * 0.6 / np.sqrt(D) * fd[:, None]).astype(np.float32),
        "query2": (n((D, Q)) * 0.6 / np.sqrt(D) * fd[:, None]).astype(np.float32),
        "query3": (n((D, Q)) * 0.6 / np.sqrt(D) * fd[:, None]).astype(np.float32),
        "keys_words": keysp[0],
        "keys_scales": keysp[1],
        "notes": (n((D, U)) / fd[:, None]).astype(np.float32),
        "pages": (n((D, Z)) / fd[:, None]).astype(np.float32),
        "old": (np.random.uniform(0.0, 2.0, (Q, M))).astype(np.float32),
        "fade": (np.random.uniform(0.3, 0.9, (Q, 1))).astype(np.float32),
        "offs": striped(idx),
        "offs2": striped(idx2),
        "offs3": striped(idx3),
        "offs4": striped(idx4),
    }


def reference(query, query2, query3, keys_words, keys_scales, notes, pages, old, fade, offs, offs2, offs3, offs4):
    idx = unstriped(offs)
    idx2 = unstriped(offs2)
    idx3 = unstriped(offs3)
    idx4 = unstriped(offs4)
    keysu = unpack_weight(keys_words, keys_scales, "e2m1")
    queryq = mxq(f64(query), 0, "e4m3")
    keysidxg = keysu[:, idx]
    query2q = mxq(f64(query2), 0, "e4m3")
    notesidx2q = mxq(f64(notes)[:, idx2], 0, "e4m3")
    query3q = mxq(f64(query3), 0, "e4m3")
    pagesidx3q = mxq(f64(pages)[:, idx3], 0, "e4m3")
    s = queryq.T @ keysidxg + query2q.T @ notesidx2q + query3q.T @ pagesidx3q
    w = sigmoid(s)
    ws = w * 2.0
    wf = np.zeros((Q, M))
    wf[:, idx4] = ws
    y = f64(old) * f64(fade) + wf
    return y

@@ -1,0 +1,170 @@
+from contextlib import ExitStack
+
+import concourse.mybir as mybir
+
+D, T, I, Q, U, Z, M = 512, 2048, 512, 128, 1024, 1024, 2048
+FLOPS = 3 * 2 * D * Q * I
+
+F32 = mybir.dt.float32
+BF16 = mybir.dt.bfloat16
+I32 = mybir.dt.int32
+U32 = mybir.dt.uint32
+U16 = mybir.dt.uint16
+U8 = mybir.dt.uint8
+FP8X4 = mybir.dt.float8_e4m3fn_x4
+FP4X4 = mybir.dt.float4_e2m1fn_x4
+ACT = mybir.ActivationFunctionType
+ALU = mybir.AluOpType
+
+P = 128
+PACK = 4
+HALF = I // 2
+QUARTER = I // 4
+LCOLS = I // 16
+HCOLS = LCOLS // 2
+WIDTHS = [256, 512, 512, 512, 256]
+
+
+def tile_attend_threesources_counts_lean_kernel(tc, query, query2, query3, keys_words, keys_scales, notes, pages,
+                                                 old, fade, offs, offs2, offs3, offs4, out):
+    nc = tc.nc
+    with ExitStack() as ctx:
+        sb = ctx.enter_context(tc.tile_pool(name="sb", bufs=1))
+        ps = ctx.enter_context(tc.psum_pool(name="ps", bufs=1))
+
+        def tile(shape, dtype, name, tag=None):
+            return sb.tile(shape, dtype, name=name, tag=tag or name, align_bytes=64)
+
+        def load(src, shape, dtype, name):
+            t = tile(shape, dtype, name)
+            nc.sync.dma_start(t[:], src)
+            return t
+
+        def half_list(lst, h):
+            return lst[:, h * HCOLS:(h + 1) * HCOLS]
+
+        key_bytes = tile([P, T], U8, "key_bytes")
+        nc.gpsimd.memset(key_bytes[:].bitcast(I32), 0)
+        placed = tile([P, M], F32, "placed")
+        nc.vector.memset(placed[:], 0.0)
+        ones = tile([P, HALF], F32, "ones")
+        nc.vector.memset(ones[:], 1.0)
+        for g in range(4):
+            nc.scalar.dma_start(key_bytes[32 * g:32 * g + 4, :].bitcast(I32),
+                                keys_scales[0, 4 * g:4 * g + 4, :].bitcast(I32))
+
+        notes_v = notes.rearrange("(p t) u -> p t u", t=PACK)
+        pages_v = pages.rearrange("(p t) u -> p t u", t=PACK)
+
+        def load_query(src, name):
+            return load(src.rearrange("(p t) q -> p t q", t=PACK), [P, PACK, Q], F32, name)
+
+        note_planes = [load(notes_v[:, 0, :], [P, U], F32, "note_plane0")]
+        list2 = load(offs2, [P, LCOLS], U16, "list2")
+        note_planes += [load(notes_v[:, 1, :], [P, U], F32, "note_plane1")]
+        list1 = load(offs, [P, LCOLS], U16, "list1")
+        note_planes += [load(notes_v[:, t, :], [P, U], F32, f"note_plane{t}") for t in range(2, PACK)]
+        q2_raw = load_query(query2, "q2_raw")
+        list3 = load(offs3, [P, LCOLS], U16, "list3")
+        page_planes = [load(pages_v[:, t, :], [P, Z], F32, f"page_plane{t}") for t in range(PACK)]
+        key_words = tile([P, T], U16, "key_words")
+        nc.sync.dma_start(key_words[:].bitcast(I32), keys_words[0].bitcast(I32))
+        q3_raw = load_query(query3, "q3_raw")
+        q1_raw = load_query(query, "q1_raw")
+        list4 = load(offs4, [P, LCOLS], U16, "list4")
+        fade_col = load(fade, [P, 1], F32, "fade_col")
+        edges = [sum(WIDTHS[:c]) for c in range(len(WIDTHS) + 1)]
+        chunks = [slice(edges[c], edges[c + 1]) for c in range(len(WIDTHS))]
+        olds = [load(old[:, cols], [P, WIDTHS[c]], F32, f"old{c}") for c, cols in enumerate(chunks)]
+
+        def gather_v(dst, window, lst):
+            nc.vector.tensor_copy(dst, window[:].indirect(lst))
+
+        def gather_s(dst, window, lst):
+            nc.scalar.activation(dst, window[:].indirect(lst), ACT.Copy)
+
+        def weave_views(dst, src):
+            return (dst.rearrange("p (c i) t -> p c t i", i=4), src.rearrange("p t (c i) -> p c t i", i=4))
+
+        def quantise(woven, n, name):
+            codes = tile([P, n], U32, name + "_codes")
+            scales = tile([P, n], U8, name + "_scales")
+            nc.vector.quantize_mx(out=codes[:].bitcast(FP8X4), scales=scales[:],
+                                  in_=woven.rearrange("p n t -> p (n t)"))
+            return codes, scales
+
+        def weave_query(raw, name):
+            woven = tile([P, Q, PACK], BF16, name)
+            dst, src = weave_views(woven[:], raw[:])
+            nc.scalar.copy(dst, src)
+            return woven
+
+        def weave(dst_tile, src_tile):
+            dst, src = weave_views(dst_tile, src_tile)
+            nc.vector.tensor_copy(dst, src)
+
+        halves = [slice(h * HALF, (h + 1) * HALF) for h in range(2)]
+        note_g = tile([P, PACK, I], BF16, "note_g")
+        key_bytes_g = tile([P, I], U8, "key_bytes_g")
+        gather_s(note_g[:, 0, :], note_planes[0], list2[:])
+        gather_v(note_g[:, 1, :], note_planes[1], list2[:])
+        gather_s(note_g[:, 2, :], note_planes[2], list2[:])
+        gather_v(key_bytes_g[:], key_bytes, list1[:])
+        gather_v(note_g[:, 3, halves[0]], note_planes[3], half_list(list2, 0))
+        gather_s(note_g[:, 3, halves[1]], note_planes[3], half_list(list2, 1))
+        note_w = tile([P, I, PACK], BF16, "note_w")
+        weave(note_w[:], note_g[:])
+        q2_w = weave_query(q2_raw, "q2_w")
+        note_c, note_s = quantise(note_w[:], I, "note")
+        q2_c, q2_s = quantise(q2_w[:], Q, "q2")
+
+        banks = [ps.tile([P, HALF], F32, name=f"bank{h}") for h in range(2)]
+
+        def product(h, q_c, q_s, codes, scales, start=False, stop=False):
+            nc.tensor.matmul_mx(out=banks[h][:], lhsT=q_c[:].bitcast(FP8X4), lhsT_scale=q_s[:],
+                                rhs=codes, rhs_scale=scales, start=start, stop=stop)
+
+        for h in range(2):
+            product(h, q2_c, q2_s, note_c[:, halves[h]].bitcast(FP8X4), note_s[:, halves[h]], start=True)
+
+        page_g = [tile([P, PACK, HALF], BF16, f"page_g{h}") for h in range(2)]
+        for t in range(PACK):
+            (gather_v if t > 0 else gather_s)(page_g[0][:, t, :], page_planes[t], half_list(list3, 0))
+            gather_s(page_g[1][:, t, :], page_planes[t], half_list(list3, 1))
+        ths = [tile([P, HALF], F32, f"tanh{h}") for h in range(2)]
+        page_w = tile([P, HALF, PACK], BF16, "page_w")
+        weave(page_w[:], page_g[0][:])
+        third_w = tile([P, QUARTER, PACK], BF16, "third_w")
+        dst, src = weave_views(third_w[:], page_g[1][:, :, 0:QUARTER])
+        nc.scalar.copy(dst, src)
+        q3_w = weave_query(q3_raw, "q3_w")
+        q1_w = weave_query(q1_raw, "q1_w")
+        page_c, page_s = quantise(page_w[:], HALF, "page0")
+        key_g0 = tile([P, HALF], U16, "key_g0")
+        gather_v(key_g0[:], key_words, half_list(list1, 0))
+        q3_c, q3_s = quantise(q3_w[:], Q, "q3")
+        q1_c, q1_s = quantise(q1_w[:], Q, "q1")
+        product(0, q3_c, q3_s, page_c[:].bitcast(FP8X4), page_s[:])
+        product(0, q1_c, q1_s, key_g0[:].bitcast(FP4X4), key_bytes_g[:, halves[0]], stop=True)
+        fourth_w = tile([P, QUARTER, PACK], BF16, "fourth_w", tag="q1_raw")
+        dst, src = weave_views(fourth_w[:], page_g[1][:, :, QUARTER:HALF])
+        nc.scalar.copy(dst, src)
+        nc.scalar.activation(ths[0][:], banks[0][:], ACT.Tanh, scale=0.5)
+        key_g1 = tile([P, HALF], U16, "key_g1", tag="q1_w")
+        gather_v(key_g1[:], key_words, half_list(list1, 1))
+        page_c = tile([P, HALF], U32, "page1_codes")
+        page_s = tile([P, HALF], U8, "page1_scales")
+        for j, woven in enumerate((third_w, fourth_w)):
+            cols = slice(j * QUARTER, (j + 1) * QUARTER)
+            nc.vector.quantize_mx(out=page_c[:, cols].bitcast(FP8X4), scales=page_s[:, cols],
+                                  in_=woven[:].rearrange("p n t -> p (n t)"))
+        product(1, q1_c, q1_s, key_g1[:].bitcast(FP4X4), key_bytes_g[:, halves[1]])
+        product(1, q3_c, q3_s, page_c[:].bitcast(FP8X4), page_s[:], stop=True)
+        nc.scalar.activation(ths[1][:], banks[1][:], ACT.Tanh, scale=0.5)
+        for h in range(2):
+            nc.vector.tensor_tensor(placed[:].indirect(half_list(list4, h)), ths[h][:], ones[:], ALU.add)
+
+        for c, cols in enumerate(chunks):
+            res = tile([P, WIDTHS[c]], F32, f"res{c}")
+            nc.vector.scalar_tensor_tensor(res[:], olds[c][:], fade_col[:], placed[:, cols], ALU.mult, ALU.add)
+            nc.sync.dma_start(out[:, cols], res[:])

@@ -44,14 +44,11 @@ def tile_attend_threesources_counts_lean_kernel(tc, query, query2, query3, keys_
             return lst[:, h * HCOLS:(h + 1) * HCOLS]
 
         key_bytes = tile([P, T], U8, "key_bytes")
-        nc.gpsimd.memset(key_bytes[:].bitcast(I32), 0)
+        nc.vector.memset(key_bytes[:].bitcast(I32), 0)
         placed = tile([P, M], F32, "placed")
         nc.vector.memset(placed[:], 0.0)
         ones = tile([P, HALF], F32, "ones")
         nc.vector.memset(ones[:], 1.0)
-        for g in range(4):
-            nc.scalar.dma_start(key_bytes[32 * g:32 * g + 4, :].bitcast(I32),
-                                keys_scales[0, 4 * g:4 * g + 4, :].bitcast(I32))
 
         notes_v = notes.rearrange("(p t) u -> p t u", t=PACK)
         pages_v = pages.rearrange("(p t) u -> p t u", t=PACK)
@@ -59,29 +56,32 @@ def tile_attend_threesources_counts_lean_kernel(tc, query, query2, query3, keys_
         def load_query(src, name):
             return load(src.rearrange("(p t) q -> p t q", t=PACK), [P, PACK, Q], F32, name)
 
-        note_planes = [load(notes_v[:, 0, :], [P, U], F32, "note_plane0")]
+        note_planes = [load(notes_v[:, 0, :], [P, U], F32, "note_plane0")[:]]
         list2 = load(offs2, [P, LCOLS], U16, "list2")
-        note_planes += [load(notes_v[:, 1, :], [P, U], F32, "note_plane1")]
+        for g in range(4):
+            nc.sync.dma_start(key_bytes[32 * g:32 * g + 4, :].bitcast(I32),
+                                keys_scales[0, 4 * g:4 * g + 4, :].bitcast(I32))
         list1 = load(offs, [P, LCOLS], U16, "list1")
-        note_planes += [load(notes_v[:, t, :], [P, U], F32, f"note_plane{t}") for t in range(2, PACK)]
-        q2_raw = load_query(query2, "q2_raw")
+        note_planes += [load(notes_v[:, t, :], [P, U], F32, f"note_plane{t}")[:] for t in range(1, PACK)]
+        page_planes = [load(pages_v[:, 0, :], [P, Z], F32, "page_plane0")[:]]
         list3 = load(offs3, [P, LCOLS], U16, "list3")
-        page_planes = [load(pages_v[:, t, :], [P, Z], F32, f"page_plane{t}") for t in range(PACK)]
+        page_planes += [load(pages_v[:, t, :], [P, Z], F32, f"page_plane{t}")[:] for t in range(1, PACK)]
+        q1_raw = load_query(query, "q1_raw")
+        q2_raw = load_query(query2, "q2_raw")
+        q3_raw = load_query(query3, "q3_raw")
         key_words = tile([P, T], U16, "key_words")
         nc.sync.dma_start(key_words[:].bitcast(I32), keys_words[0].bitcast(I32))
-        q3_raw = load_query(query3, "q3_raw")
-        q1_raw = load_query(query, "q1_raw")
         list4 = load(offs4, [P, LCOLS], U16, "list4")
         fade_col = load(fade, [P, 1], F32, "fade_col")
         edges = [sum(WIDTHS[:c]) for c in range(len(WIDTHS) + 1)]
         chunks = [slice(edges[c], edges[c + 1]) for c in range(len(WIDTHS))]
-        olds = [load(old[:, cols], [P, WIDTHS[c]], F32, f"old{c}") for c, cols in enumerate(chunks)]
+        old_sb = load(old, [P, M], F32, "old_sb")
 
         def gather_v(dst, window, lst):
-            nc.vector.tensor_copy(dst, window[:].indirect(lst))
+            nc.vector.tensor_copy(dst, window.indirect(lst))
 
         def gather_s(dst, window, lst):
-            nc.scalar.activation(dst, window[:].indirect(lst), ACT.Copy)
+            nc.scalar.activation(dst, window.indirect(lst), ACT.Copy)
 
         def weave_views(dst, src):
             return (dst.rearrange("p (c i) t -> p c t i", i=4), src.rearrange("p t (c i) -> p c t i", i=4))
@@ -104,67 +104,64 @@ def tile_attend_threesources_counts_lean_kernel(tc, query, query2, query3, keys_
             nc.vector.tensor_copy(dst, src)
 
         halves = [slice(h * HALF, (h + 1) * HALF) for h in range(2)]
-        note_g = tile([P, PACK, I], BF16, "note_g")
+        note_g = [tile([P, PACK, HALF], BF16, f"note_g{h}") for h in range(2)]
         key_bytes_g = tile([P, I], U8, "key_bytes_g")
-        gather_s(note_g[:, 0, :], note_planes[0], list2[:])
-        gather_v(note_g[:, 1, :], note_planes[1], list2[:])
-        gather_s(note_g[:, 2, :], note_planes[2], list2[:])
-        gather_v(key_bytes_g[:], key_bytes, list1[:])
-        gather_v(note_g[:, 3, halves[0]], note_planes[3], half_list(list2, 0))
-        gather_s(note_g[:, 3, halves[1]], note_planes[3], half_list(list2, 1))
-        note_w = tile([P, I, PACK], BF16, "note_w")
-        weave(note_w[:], note_g[:])
-        q2_w = weave_query(q2_raw, "q2_w")
-        note_c, note_s = quantise(note_w[:], I, "note")
-        q2_c, q2_s = quantise(q2_w[:], Q, "q2")
-
-        banks = [ps.tile([P, HALF], F32, name=f"bank{h}") for h in range(2)]
-
-        def product(h, q_c, q_s, codes, scales, start=False, stop=False):
-            nc.tensor.matmul_mx(out=banks[h][:], lhsT=q_c[:].bitcast(FP8X4), lhsT_scale=q_s[:],
-                                rhs=codes, rhs_scale=scales, start=start, stop=stop)
-
-        for h in range(2):
-            product(h, q2_c, q2_s, note_c[:, halves[h]].bitcast(FP8X4), note_s[:, halves[h]], start=True)
+        for t in range(PACK):
+            gather_v(note_g[0][:, t, :], note_planes[t], half_list(list2, 0))
+            gather_s(note_g[1][:, t, :], note_planes[t], half_list(list2, 1))
+            if t == 0:
+                gather_v(key_bytes_g[:], key_bytes[:], list1[:])
+        note_w = [tile([P, HALF, PACK], BF16, f"note_w{h}") for h in range(2)]
+        weave(note_w[0][:], note_g[0][:])
+        dst, src = weave_views(note_w[1][:], note_g[1][:])
+        nc.scalar.copy(dst, src)
+        note_q = [quantise(note_w[h][:], HALF, f"note{h}") for h in range(2)]
 
         page_g = [tile([P, PACK, HALF], BF16, f"page_g{h}") for h in range(2)]
         for t in range(PACK):
-            (gather_v if t > 0 else gather_s)(page_g[0][:, t, :], page_planes[t], half_list(list3, 0))
+            gather_v(page_g[0][:, t, :], page_planes[t], half_list(list3, 0))
             gather_s(page_g[1][:, t, :], page_planes[t], half_list(list3, 1))
-        ths = [tile([P, HALF], F32, f"tanh{h}") for h in range(2)]
-        page_w = tile([P, HALF, PACK], BF16, "page_w")
-        weave(page_w[:], page_g[0][:])
-        third_w = tile([P, QUARTER, PACK], BF16, "third_w")
-        dst, src = weave_views(third_w[:], page_g[1][:, :, 0:QUARTER])
-        nc.scalar.copy(dst, src)
-        q3_w = weave_query(q3_raw, "q3_w")
+        page_w0 = tile([P, HALF, PACK], BF16, "page_w0")
+        weave(page_w0[:], page_g[0][:])
         q1_w = weave_query(q1_raw, "q1_w")
-        page_c, page_s = quantise(page_w[:], HALF, "page0")
-        key_g0 = tile([P, HALF], U16, "key_g0")
-        gather_v(key_g0[:], key_words, half_list(list1, 0))
-        q3_c, q3_s = quantise(q3_w[:], Q, "q3")
+        q2_w = weave_query(q2_raw, "q2_w")
+        page_c0, page_s0 = quantise(page_w0[:], HALF, "page0")
+        q3_w = tile([P, Q, PACK], BF16, "q3_w")
+        weave(q3_w[:], q3_raw[:])
         q1_c, q1_s = quantise(q1_w[:], Q, "q1")
-        product(0, q3_c, q3_s, page_c[:].bitcast(FP8X4), page_s[:])
-        product(0, q1_c, q1_s, key_g0[:].bitcast(FP4X4), key_bytes_g[:, halves[0]], stop=True)
-        fourth_w = tile([P, QUARTER, PACK], BF16, "fourth_w", tag="q1_raw")
-        dst, src = weave_views(fourth_w[:], page_g[1][:, :, QUARTER:HALF])
-        nc.scalar.copy(dst, src)
-        nc.scalar.activation(ths[0][:], banks[0][:], ACT.Tanh, scale=0.5)
-        key_g1 = tile([P, HALF], U16, "key_g1", tag="q1_w")
-        gather_v(key_g1[:], key_words, half_list(list1, 1))
-        page_c = tile([P, HALF], U32, "page1_codes")
-        page_s = tile([P, HALF], U8, "page1_scales")
-        for j, woven in enumerate((third_w, fourth_w)):
-            cols = slice(j * QUARTER, (j + 1) * QUARTER)
-            nc.vector.quantize_mx(out=page_c[:, cols].bitcast(FP8X4), scales=page_s[:, cols],
-                                  in_=woven[:].rearrange("p n t -> p (n t)"))
-        product(1, q1_c, q1_s, key_g1[:].bitcast(FP4X4), key_bytes_g[:, halves[1]])
-        product(1, q3_c, q3_s, page_c[:].bitcast(FP8X4), page_s[:], stop=True)
-        nc.scalar.activation(ths[1][:], banks[1][:], ACT.Tanh, scale=0.5)
+        q2_c, q2_s = quantise(q2_w[:], Q, "q2")
+        q3_c, q3_s = quantise(q3_w[:], Q, "q3")
+        key_g = [tile([P, HALF], U16, f"key_g{h}") for h in range(2)]
         for h in range(2):
-            nc.vector.tensor_tensor(placed[:].indirect(half_list(list4, h)), ths[h][:], ones[:], ALU.add)
+            gather_v(key_g[h][:], key_words[:], half_list(list1, h))
+        page_w1 = tile([P, HALF, PACK], BF16, "page_w1", tag="q2_raw")
+        dst, src = weave_views(page_w1[:], page_g[1][:])
+        nc.scalar.copy(dst, src)
+        page_c1, page_s1 = quantise(page_w1[:], HALF, "page1")
+
+        runs = [slice(0, QUARTER), slice(QUARTER, HALF), slice(HALF, I)]
+        banks = [ps.tile([P, r.stop - r.start], F32, name=f"bank{j}") for j, r in enumerate(runs)]
+
+        def product(j, q_c, q_s, codes, scales, start=False, stop=False):
+            nc.tensor.matmul_mx(out=banks[j][:], lhsT=q_c[:].bitcast(FP8X4), lhsT_scale=q_s[:],
+                                rhs=codes, rhs_scale=scales, start=start, stop=stop)
+
+        for j, r in enumerate(runs[:2]):
+            product(j, q2_c, q2_s, note_q[0][0][:, r].bitcast(FP8X4), note_q[0][1][:, r], start=True)
+        product(2, q2_c, q2_s, note_q[1][0][:].bitcast(FP8X4), note_q[1][1][:], start=True)
+        for j, r in enumerate(runs[:2]):
+            product(j, q3_c, q3_s, page_c0[:, r].bitcast(FP8X4), page_s0[:, r])
+        for j, r in enumerate(runs[:2]):
+            product(j, q1_c, q1_s, key_g[0][:, r].bitcast(FP4X4), key_bytes_g[:, r], stop=True)
+        product(2, q1_c, q1_s, key_g[1][:].bitcast(FP4X4), key_bytes_g[:, runs[2]])
+        product(2, q3_c, q3_s, page_c1[:].bitcast(FP8X4), page_s1[:], stop=True)
+        for j, r in enumerate(runs):
+            th = tile([P, r.stop - r.start], F32, f"tanh{j}")
+            nc.scalar.activation(th[:], banks[j][:], ACT.Tanh, scale=0.5)
+            nc.vector.tensor_tensor(placed[:].indirect(list4[:, r.start // 16:r.stop // 16]), th[:],
+                                    ones[:, 0:r.stop - r.start], ALU.add)
 
         for c, cols in enumerate(chunks):
             res = tile([P, WIDTHS[c]], F32, f"res{c}")
-            nc.vector.scalar_tensor_tensor(res[:], olds[c][:], fade_col[:], placed[:, cols], ALU.mult, ALU.add)
+            nc.vector.scalar_tensor_tensor(res[:], old_sb[:, cols], fade_col[:], placed[:, cols], ALU.mult, ALU.add)
             nc.sync.dma_start(out[:, cols], res[:])

@@ -47,7 +47,7 @@ def tile_attend_threesources_counts_lean_kernel(tc, query, query2, query3, keys_
         nc.vector.memset(key_bytes[:].bitcast(I32), 0)
         placed = tile([P, M], F32, "placed")
         nc.vector.memset(placed[:], 0.0)
-        ones = tile([P, HALF], F32, "ones")
+        ones = tile([P, I - QUARTER], F32, "ones")
         nc.vector.memset(ones[:], 1.0)
 
         notes_v = notes.rearrange("(p t) u -> p t u", t=PACK)
@@ -56,8 +56,8 @@ def tile_attend_threesources_counts_lean_kernel(tc, query, query2, query3, keys_
         def load_query(src, name):
             return load(src.rearrange("(p t) q -> p t q", t=PACK), [P, PACK, Q], F32, name)
 
-        note_planes = [load(notes_v[:, 0, :], [P, U], F32, "note_plane0")[:]]
         list2 = load(offs2, [P, LCOLS], U16, "list2")
+        note_planes = [load(notes_v[:, 0, :], [P, U], F32, "note_plane0")[:]]
         for g in range(4):
             nc.sync.dma_start(key_bytes[32 * g:32 * g + 4, :].bitcast(I32),
                                 keys_scales[0, 4 * g:4 * g + 4, :].bitcast(I32))
@@ -66,9 +66,9 @@ def tile_attend_threesources_counts_lean_kernel(tc, query, query2, query3, keys_
         page_planes = [load(pages_v[:, 0, :], [P, Z], F32, "page_plane0")[:]]
         list3 = load(offs3, [P, LCOLS], U16, "list3")
         page_planes += [load(pages_v[:, t, :], [P, Z], F32, f"page_plane{t}")[:] for t in range(1, PACK)]
-        q1_raw = load_query(query, "q1_raw")
         q2_raw = load_query(query2, "q2_raw")
         q3_raw = load_query(query3, "q3_raw")
+        q1_raw = load_query(query, "q1_raw")
         key_words = tile([P, T], U16, "key_words")
         nc.sync.dma_start(key_words[:].bitcast(I32), keys_words[0].bitcast(I32))
         list4 = load(offs4, [P, LCOLS], U16, "list4")
@@ -86,18 +86,12 @@ def tile_attend_threesources_counts_lean_kernel(tc, query, query2, query3, keys_
         def weave_views(dst, src):
             return (dst.rearrange("p (c i) t -> p c t i", i=4), src.rearrange("p t (c i) -> p c t i", i=4))
 
-        def quantise(woven, n, name):
-            codes = tile([P, n], U32, name + "_codes")
+        def quantise(woven, n, name, tag=None):
+            codes = tile([P, n], U32, name + "_codes", tag)
             scales = tile([P, n], U8, name + "_scales")
             nc.vector.quantize_mx(out=codes[:].bitcast(FP8X4), scales=scales[:],
                                   in_=woven.rearrange("p n t -> p (n t)"))
             return codes, scales
-
-        def weave_query(raw, name):
-            woven = tile([P, Q, PACK], BF16, name)
-            dst, src = weave_views(woven[:], raw[:])
-            nc.scalar.copy(dst, src)
-            return woven
 
         def weave(dst_tile, src_tile):
             dst, src = weave_views(dst_tile, src_tile)
@@ -123,27 +117,31 @@ def tile_attend_threesources_counts_lean_kernel(tc, query, query2, query3, keys_
             gather_s(page_g[1][:, t, :], page_planes[t], half_list(list3, 1))
         page_w0 = tile([P, HALF, PACK], BF16, "page_w0")
         weave(page_w0[:], page_g[0][:])
-        q1_w = weave_query(q1_raw, "q1_w")
-        q2_w = weave_query(q2_raw, "q2_w")
+        q2_w = tile([P, Q, PACK], BF16, "q2_w")
+        weave(q2_w[:], q2_raw[:])
+        q31_w = tile([P, 2 * Q, PACK], BF16, "q31_w")
+        for j, raw in enumerate((q3_raw, q1_raw)):
+            dst, src = weave_views(q31_w[:, j * Q:(j + 1) * Q, :], raw[:])
+            nc.scalar.copy(dst, src)
         page_c0, page_s0 = quantise(page_w0[:], HALF, "page0")
-        q3_w = tile([P, Q, PACK], BF16, "q3_w")
-        weave(q3_w[:], q3_raw[:])
-        q1_c, q1_s = quantise(q1_w[:], Q, "q1")
         q2_c, q2_s = quantise(q2_w[:], Q, "q2")
-        q3_c, q3_s = quantise(q3_w[:], Q, "q3")
+        q31_c, q31_s = quantise(q31_w[:], 2 * Q, "q31")
+        q2_c, q2_s = q2_c[:], q2_s[:]
+        q3_c, q3_s = q31_c[:, 0:Q], q31_s[:, 0:Q]
+        q1_c, q1_s = q31_c[:, Q:2 * Q], q31_s[:, Q:2 * Q]
         key_g = [tile([P, HALF], U16, f"key_g{h}") for h in range(2)]
         for h in range(2):
             gather_v(key_g[h][:], key_words[:], half_list(list1, h))
-        page_w1 = tile([P, HALF, PACK], BF16, "page_w1", tag="q2_raw")
+        page_w1 = tile([P, HALF, PACK], BF16, "page_w1", tag="q1_raw")
         dst, src = weave_views(page_w1[:], page_g[1][:])
         nc.scalar.copy(dst, src)
-        page_c1, page_s1 = quantise(page_w1[:], HALF, "page1")
+        page_c1, page_s1 = quantise(page_w1[:], HALF, "page1", tag="key_words")
 
         runs = [slice(0, QUARTER), slice(QUARTER, HALF), slice(HALF, I)]
         banks = [ps.tile([P, r.stop - r.start], F32, name=f"bank{j}") for j, r in enumerate(runs)]
 
         def product(j, q_c, q_s, codes, scales, start=False, stop=False):
-            nc.tensor.matmul_mx(out=banks[j][:], lhsT=q_c[:].bitcast(FP8X4), lhsT_scale=q_s[:],
+            nc.tensor.matmul_mx(out=banks[j][:], lhsT=q_c.bitcast(FP8X4), lhsT_scale=q_s,
                                 rhs=codes, rhs_scale=scales, start=start, stop=stop)
 
         for j, r in enumerate(runs[:2]):
@@ -155,11 +153,13 @@ def tile_attend_threesources_counts_lean_kernel(tc, query, query2, query3, keys_
             product(j, q1_c, q1_s, key_g[0][:, r].bitcast(FP4X4), key_bytes_g[:, r], stop=True)
         product(2, q1_c, q1_s, key_g[1][:].bitcast(FP4X4), key_bytes_g[:, runs[2]])
         product(2, q3_c, q3_s, page_c1[:].bitcast(FP8X4), page_s1[:], stop=True)
-        for j, r in enumerate(runs):
-            th = tile([P, r.stop - r.start], F32, f"tanh{j}")
-            nc.scalar.activation(th[:], banks[j][:], ACT.Tanh, scale=0.5)
-            nc.vector.tensor_tensor(placed[:].indirect(list4[:, r.start // 16:r.stop // 16]), th[:],
-                                    ones[:, 0:r.stop - r.start], ALU.add)
+        first = tile([P, QUARTER], F32, "tanh_first")
+        rest = tile([P, I - QUARTER], F32, "tanh_rest")
+        nc.scalar.activation(first[:], banks[0][:], ACT.Tanh, scale=0.5)
+        nc.scalar.activation(rest[:, 0:QUARTER], banks[1][:], ACT.Tanh, scale=0.5)
+        nc.scalar.activation(rest[:, QUARTER:], banks[2][:], ACT.Tanh, scale=0.5)
+        nc.vector.tensor_tensor(placed[:].indirect(list4[:, 0:QUARTER // 16]), first[:], ones[:, 0:QUARTER], ALU.add)
+        nc.vector.tensor_tensor(placed[:].indirect(list4[:, QUARTER // 16:]), rest[:], ones[:], ALU.add)
 
         for c, cols in enumerate(chunks):
             res = tile([P, WIDTHS[c]], F32, f"res{c}")

@@ -45,6 +45,8 @@ def tile_attend_threesources_counts_lean_kernel(tc, query, query2, query3, keys_
 
         key_bytes = tile([P, T], U8, "key_bytes")
         nc.vector.memset(key_bytes[:].bitcast(I32), 0)
+        key_plane = tile([P, I], U8, "key_plane")
+        nc.vector.memset(key_plane[:].bitcast(I32), 0)
         placed = tile([P, M], F32, "placed")
         nc.vector.memset(placed[:], 0.0)
         ones = tile([P, I - QUARTER], F32, "ones")
@@ -56,16 +58,21 @@ def tile_attend_threesources_counts_lean_kernel(tc, query, query2, query3, keys_
         def load_query(src, name):
             return load(src.rearrange("(p t) q -> p t q", t=PACK), [P, PACK, Q], F32, name)
 
+        note_first = load(notes_v[:, 0, :], [P, U], F32, "note_first")
         list2 = load(offs2, [P, LCOLS], U16, "list2")
-        note_planes = [load(notes_v[:, 0, :], [P, U], F32, "note_plane0")[:]]
-        for g in range(4):
-            nc.sync.dma_start(key_bytes[32 * g:32 * g + 4, :].bitcast(I32),
-                                keys_scales[0, 4 * g:4 * g + 4, :].bitcast(I32))
         list1 = load(offs, [P, LCOLS], U16, "list1")
-        note_planes += [load(notes_v[:, t, :], [P, U], F32, f"note_plane{t}")[:] for t in range(1, PACK)]
-        page_planes = [load(pages_v[:, 0, :], [P, Z], F32, "page_plane0")[:]]
+        nc.sync.dma_start(key_bytes[0:P:8, :].bitcast(I32), keys_scales[0].bitcast(I32))
+        note_pair = load(notes_v[:, 1:3, :], [P, 2, U], F32, "note_pair")
+        note_last = load(notes_v[:, 3, :], [P, U], F32, "note_last")
+        note_planes = [note_first[:], note_pair[:, 0, :], note_pair[:, 1, :], note_last[:]]
+        page_pair = load(pages_v[:, 0:2, :], [P, 2, Z], F32, "page_pair")
         list3 = load(offs3, [P, LCOLS], U16, "list3")
-        page_planes += [load(pages_v[:, t, :], [P, Z], F32, f"page_plane{t}")[:] for t in range(1, PACK)]
+        key_bytes_g = tile([P, I], U8, "key_bytes_g")
+        nc.vector.tensor_copy(key_bytes_g[:], key_bytes[:].indirect(list1[:]))
+        for r in range(4):
+            nc.sync.dma_start(key_plane[r:P:32, :].bitcast(I32), key_bytes_g[8 * r:P:32, :].bitcast(I32))
+        page_planes = [page_pair[:, 0, :], page_pair[:, 1, :]]
+        page_planes += [load(pages_v[:, t, :], [P, Z], F32, f"page_plane{t}")[:] for t in range(2, PACK)]
         q2_raw = load_query(query2, "q2_raw")
         q3_raw = load_query(query3, "q3_raw")
         q1_raw = load_query(query, "q1_raw")
@@ -86,8 +93,8 @@ def tile_attend_threesources_counts_lean_kernel(tc, query, query2, query3, keys_
         def weave_views(dst, src):
             return (dst.rearrange("p (c i) t -> p c t i", i=4), src.rearrange("p t (c i) -> p c t i", i=4))
 
-        def quantise(woven, n, name, tag=None):
-            codes = tile([P, n], U32, name + "_codes", tag)
+        def quantise(woven, n, name):
+            codes = tile([P, n], U32, name + "_codes")
             scales = tile([P, n], U8, name + "_scales")
             nc.vector.quantize_mx(out=codes[:].bitcast(FP8X4), scales=scales[:],
                                   in_=woven.rearrange("p n t -> p (n t)"))
@@ -97,21 +104,17 @@ def tile_attend_threesources_counts_lean_kernel(tc, query, query2, query3, keys_
             dst, src = weave_views(dst_tile, src_tile)
             nc.vector.tensor_copy(dst, src)
 
-        halves = [slice(h * HALF, (h + 1) * HALF) for h in range(2)]
-        note_g = [tile([P, PACK, HALF], BF16, f"note_g{h}") for h in range(2)]
-        key_bytes_g = tile([P, I], U8, "key_bytes_g")
+        note_g = [tile([P, PACK, HALF], F32, f"note_g{h}") for h in range(2)]
         for t in range(PACK):
             gather_v(note_g[0][:, t, :], note_planes[t], half_list(list2, 0))
-            gather_s(note_g[1][:, t, :], note_planes[t], half_list(list2, 1))
-            if t == 0:
-                gather_v(key_bytes_g[:], key_bytes[:], list1[:])
+            (gather_v if t == 1 else gather_s)(note_g[1][:, t, :], note_planes[t], half_list(list2, 1))
         note_w = [tile([P, HALF, PACK], BF16, f"note_w{h}") for h in range(2)]
         weave(note_w[0][:], note_g[0][:])
         dst, src = weave_views(note_w[1][:], note_g[1][:])
         nc.scalar.copy(dst, src)
         note_q = [quantise(note_w[h][:], HALF, f"note{h}") for h in range(2)]
 
-        page_g = [tile([P, PACK, HALF], BF16, f"page_g{h}") for h in range(2)]
+        page_g = [tile([P, PACK, HALF], F32, f"page_g{h}") for h in range(2)]
         for t in range(PACK):
             gather_v(page_g[0][:, t, :], page_planes[t], half_list(list3, 0))
             gather_s(page_g[1][:, t, :], page_planes[t], half_list(list3, 1))
@@ -135,7 +138,7 @@ def tile_attend_threesources_counts_lean_kernel(tc, query, query2, query3, keys_
         page_w1 = tile([P, HALF, PACK], BF16, "page_w1", tag="q1_raw")
         dst, src = weave_views(page_w1[:], page_g[1][:])
         nc.scalar.copy(dst, src)
-        page_c1, page_s1 = quantise(page_w1[:], HALF, "page1", tag="key_words")
+        page_c1, page_s1 = quantise(page_w1[:], HALF, "page1")
 
         runs = [slice(0, QUARTER), slice(QUARTER, HALF), slice(HALF, I)]
         banks = [ps.tile([P, r.stop - r.start], F32, name=f"bank{j}") for j, r in enumerate(runs)]
@@ -150,9 +153,9 @@ def tile_attend_threesources_counts_lean_kernel(tc, query, query2, query3, keys_
         for j, r in enumerate(runs[:2]):
             product(j, q3_c, q3_s, page_c0[:, r].bitcast(FP8X4), page_s0[:, r])
         for j, r in enumerate(runs[:2]):
-            product(j, q1_c, q1_s, key_g[0][:, r].bitcast(FP4X4), key_bytes_g[:, r], stop=True)
-        product(2, q1_c, q1_s, key_g[1][:].bitcast(FP4X4), key_bytes_g[:, runs[2]])
-        product(2, q3_c, q3_s, page_c1[:].bitcast(FP8X4), page_s1[:], stop=True)
+            product(j, q1_c, q1_s, key_g[0][:, r].bitcast(FP4X4), key_plane[:, r], stop=True)
+        product(2, q3_c, q3_s, page_c1[:].bitcast(FP8X4), page_s1[:])
+        product(2, q1_c, q1_s, key_g[1][:].bitcast(FP4X4), key_plane[:, runs[2]], stop=True)
         first = tile([P, QUARTER], F32, "tanh_first")
         rest = tile([P, I - QUARTER], F32, "tanh_rest")
         nc.scalar.activation(first[:], banks[0][:], ACT.Tanh, scale=0.5)

from contextlib import ExitStack

import concourse.mybir as mybir

D, T, I, Q, U, Z, M = 512, 2048, 512, 128, 1024, 1024, 2048
FLOPS = 3 * 2 * D * Q * I

F32 = mybir.dt.float32
BF16 = mybir.dt.bfloat16
I32 = mybir.dt.int32
U32 = mybir.dt.uint32
U16 = mybir.dt.uint16
U8 = mybir.dt.uint8
FP8X4 = mybir.dt.float8_e4m3fn_x4
FP4X4 = mybir.dt.float4_e2m1fn_x4
ACT = mybir.ActivationFunctionType
ALU = mybir.AluOpType

P = 128
PACK = 4
HALF = I // 2
QUARTER = I // 4
LCOLS = I // 16
HCOLS = LCOLS // 2
WIDTHS = [256, 512, 512, 512, 256]


def tile_attend_threesources_counts_lean_kernel(tc, query, query2, query3, keys_words, keys_scales, notes, pages,
                                                 old, fade, offs, offs2, offs3, offs4, out):
    nc = tc.nc
    with ExitStack() as ctx:
        sb = ctx.enter_context(tc.tile_pool(name="sb", bufs=1))
        ps = ctx.enter_context(tc.psum_pool(name="ps", bufs=1))

        def tile(shape, dtype, name, tag=None):
            return sb.tile(shape, dtype, name=name, tag=tag or name, align_bytes=64)

        def load(src, shape, dtype, name):
            t = tile(shape, dtype, name)
            nc.sync.dma_start(t[:], src)
            return t

        def half_list(lst, h):
            return lst[:, h * HCOLS:(h + 1) * HCOLS]

        key_bytes = tile([P, T], U8, "key_bytes")
        nc.vector.memset(key_bytes[:].bitcast(I32), 0)
        key_plane = tile([P, I], U8, "key_plane")
        nc.vector.memset(key_plane[:].bitcast(I32), 0)
        placed = tile([P, M], F32, "placed")
        nc.vector.memset(placed[:], 0.0)
        ones = tile([P, I - QUARTER], F32, "ones")
        nc.vector.memset(ones[:], 1.0)

        notes_v = notes.rearrange("(p t) u -> p t u", t=PACK)
        pages_v = pages.rearrange("(p t) u -> p t u", t=PACK)

        def load_query(src, name):
            return load(src.rearrange("(p t) q -> p t q", t=PACK), [P, PACK, Q], F32, name)

        note_first = load(notes_v[:, 0, :], [P, U], F32, "note_first")
        list2 = load(offs2, [P, LCOLS], U16, "list2")
        list1 = load(offs, [P, LCOLS], U16, "list1")
        nc.sync.dma_start(key_bytes[0:P:8, :].bitcast(I32), keys_scales[0].bitcast(I32))
        note_pair = load(notes_v[:, 1:3, :], [P, 2, U], F32, "note_pair")
        note_last = load(notes_v[:, 3, :], [P, U], F32, "note_last")
        note_planes = [note_first[:], note_pair[:, 0, :], note_pair[:, 1, :], note_last[:]]
        page_pair = load(pages_v[:, 0:2, :], [P, 2, Z], F32, "page_pair")
        list3 = load(offs3, [P, LCOLS], U16, "list3")
        key_bytes_g = tile([P, I], U8, "key_bytes_g")
        nc.vector.tensor_copy(key_bytes_g[:], key_bytes[:].indirect(list1[:]))
        for r in range(4):
            nc.sync.dma_start(key_plane[r:P:32, :].bitcast(I32), key_bytes_g[8 * r:P:32, :].bitcast(I32))
        page_planes = [page_pair[:, 0, :], page_pair[:, 1, :]]
        page_planes += [load(pages_v[:, t, :], [P, Z], F32, f"page_plane{t}")[:] for t in range(2, PACK)]
        q2_raw = load_query(query2, "q2_raw")
        q3_raw = load_query(query3, "q3_raw")
        q1_raw = load_query(query, "q1_raw")
        key_words = tile([P, T], U16, "key_words")
        nc.sync.dma_start(key_words[:].bitcast(I32), keys_words[0].bitcast(I32))
        list4 = load(offs4, [P, LCOLS], U16, "list4")
        fade_col = load(fade, [P, 1], F32, "fade_col")
        edges = [sum(WIDTHS[:c]) for c in range(len(WIDTHS) + 1)]
        chunks = [slice(edges[c], edges[c + 1]) for c in range(len(WIDTHS))]
        old_sb = load(old, [P, M], F32, "old_sb")

        def gather_v(dst, window, lst):
            nc.vector.tensor_copy(dst, window.indirect(lst))

        def gather_s(dst, window, lst):
            nc.scalar.activation(dst, window.indirect(lst), ACT.Copy)

        def weave_views(dst, src):
            return (dst.rearrange("p (c i) t -> p c t i", i=4), src.rearrange("p t (c i) -> p c t i", i=4))

        def quantise(woven, n, name):
            codes = tile([P, n], U32, name + "_codes")
            scales = tile([P, n], U8, name + "_scales")
            nc.vector.quantize_mx(out=codes[:].bitcast(FP8X4), scales=scales[:],
                                  in_=woven.rearrange("p n t -> p (n t)"))
            return codes, scales

        def weave(dst_tile, src_tile):
            dst, src = weave_views(dst_tile, src_tile)
            nc.vector.tensor_copy(dst, src)

        note_g = [tile([P, PACK, HALF], F32, f"note_g{h}") for h in range(2)]
        for t in range(PACK):
            gather_v(note_g[0][:, t, :], note_planes[t], half_list(list2, 0))
            (gather_v if t == 1 else gather_s)(note_g[1][:, t, :], note_planes[t], half_list(list2, 1))
        note_w = [tile([P, HALF, PACK], BF16, f"note_w{h}") for h in range(2)]
        weave(note_w[0][:], note_g[0][:])
        dst, src = weave_views(note_w[1][:], note_g[1][:])
        nc.scalar.copy(dst, src)
        note_q = [quantise(note_w[h][:], HALF, f"note{h}") for h in range(2)]

        page_g = [tile([P, PACK, HALF], F32, f"page_g{h}") for h in range(2)]
        for t in range(PACK):
            gather_v(page_g[0][:, t, :], page_planes[t], half_list(list3, 0))
            gather_s(page_g[1][:, t, :], page_planes[t], half_list(list3, 1))
        page_w0 = tile([P, HALF, PACK], BF16, "page_w0")
        weave(page_w0[:], page_g[0][:])
        q2_w = tile([P, Q, PACK], BF16, "q2_w")
        weave(q2_w[:], q2_raw[:])
        q31_w = tile([P, 2 * Q, PACK], BF16, "q31_w")
        for j, raw in enumerate((q3_raw, q1_raw)):
            dst, src = weave_views(q31_w[:, j * Q:(j + 1) * Q, :], raw[:])
            nc.scalar.copy(dst, src)
        page_c0, page_s0 = quantise(page_w0[:], HALF, "page0")
        q2_c, q2_s = quantise(q2_w[:], Q, "q2")
        q31_c, q31_s = quantise(q31_w[:], 2 * Q, "q31")
        q2_c, q2_s = q2_c[:], q2_s[:]
        q3_c, q3_s = q31_c[:, 0:Q], q31_s[:, 0:Q]
        q1_c, q1_s = q31_c[:, Q:2 * Q], q31_s[:, Q:2 * Q]
        key_g = [tile([P, HALF], U16, f"key_g{h}") for h in range(2)]
        for h in range(2):
            gather_v(key_g[h][:], key_words[:], half_list(list1, h))
        page_w1 = tile([P, HALF, PACK], BF16, "page_w1", tag="q1_raw")
        dst, src = weave_views(page_w1[:], page_g[1][:])
        nc.scalar.copy(dst, src)
        page_c1, page_s1 = quantise(page_w1[:], HALF, "page1")

        runs = [slice(0, QUARTER), slice(QUARTER, HALF), slice(HALF, I)]
        banks = [ps.tile([P, r.stop - r.start], F32, name=f"bank{j}") for j, r in enumerate(runs)]

        def product(j, q_c, q_s, codes, scales, start=False, stop=False):
            nc.tensor.matmul_mx(out=banks[j][:], lhsT=q_c.bitcast(FP8X4), lhsT_scale=q_s,
                                rhs=codes, rhs_scale=scales, start=start, stop=stop)

        for j, r in enumerate(runs[:2]):
            product(j, q2_c, q2_s, note_q[0][0][:, r].bitcast(FP8X4), note_q[0][1][:, r], start=True)
        product(2, q2_c, q2_s, note_q[1][0][:].bitcast(FP8X4), note_q[1][1][:], start=True)
        for j, r in enumerate(runs[:2]):
            product(j, q3_c, q3_s, page_c0[:, r].bitcast(FP8X4), page_s0[:, r])
        for j, r in enumerate(runs[:2]):
            product(j, q1_c, q1_s, key_g[0][:, r].bitcast(FP4X4), key_plane[:, r], stop=True)
        product(2, q3_c, q3_s, page_c1[:].bitcast(FP8X4), page_s1[:])
        product(2, q1_c, q1_s, key_g[1][:].bitcast(FP4X4), key_plane[:, runs[2]], stop=True)
        first = tile([P, QUARTER], F32, "tanh_first")
        rest = tile([P, I - QUARTER], F32, "tanh_rest")
        nc.scalar.activation(first[:], banks[0][:], ACT.Tanh, scale=0.5)
        nc.scalar.activation(rest[:, 0:QUARTER], banks[1][:], ACT.Tanh, scale=0.5)
        nc.scalar.activation(rest[:, QUARTER:], banks[2][:], ACT.Tanh, scale=0.5)
        nc.vector.tensor_tensor(placed[:].indirect(list4[:, 0:QUARTER // 16]), first[:], ones[:, 0:QUARTER], ALU.add)
        nc.vector.tensor_tensor(placed[:].indirect(list4[:, QUARTER // 16:]), rest[:], ones[:], ALU.add)

        for c, cols in enumerate(chunks):
            res = tile([P, WIDTHS[c]], F32, f"res{c}")
            nc.vector.scalar_tensor_tensor(res[:], old_sb[:, cols], fade_col[:], placed[:, cols], ALU.mult, ALU.add)
            nc.sync.dma_start(out[:, cols], res[:])
